import numpy as np
import ml_dtypes


def mxq(x, axis, fmt="e4m3"):
    dtype, down = {"e4m3": (ml_dtypes.float8_e4m3fn, 7), "e5m2": (ml_dtypes.float8_e5m2, 14)}[fmt]
    v = np.moveaxis(np.asarray(x, np.float32).astype(ml_dtypes.bfloat16).astype(np.float64), axis, -1)
    blocks = v.reshape(v.shape[:-1] + (-1, 32))
    amax = np.abs(blocks).max(-1, keepdims=True)
    byte = np.maximum(np.where(amax > 0, np.frexp(amax)[1] - 1 + 127, 0) - down, 1)
    scale = np.exp2(byte - 127.0)
    codes = (blocks / scale).astype(np.float32).astype(dtype).astype(np.float64)
    return np.moveaxis((codes * scale).reshape(v.shape), -1, axis)


WIDE = False


def mx_kscale(k):
    if not WIDE:
        return np.ones(k)
    levels = np.array([10, -10, 5, -5, 0])
    if k % 512:
        return np.exp2(np.random.permutation(np.resize(levels, k // 32))).repeat(32)
    a = np.empty((k // 512, 16))
    for p in range(k // 512):
        a[p, :8] = np.random.permutation(np.resize(levels, 8))
        for g in range(8):
            far = levels[np.abs(levels - a[p, g]) >= 10]
            a[p, g + 8] = far[np.random.randint(len(far))]
    return np.exp2(a.ravel()).repeat(32)


def f64(x):
    return np.asarray(x).astype(np.float64)


def striped(idx):
    return np.tile(idx.reshape(-1, 16).T, (8, 1)).astype(np.uint16)


def unstriped(offs):
    return offs[:16].T.reshape(-1).astype(np.int64)


def striped8(idx):
    return np.concatenate([x.reshape(-1, 16).T for x in idx]).astype(np.uint16)


def runs(offs, k):
    lists = np.stack([offs[16 * r : 16 * r + 16].T.reshape(-1) for r in range(8)]).astype(np.int64)
    return lists[np.arange(k) % 512 // 64]


def pack_weight(w):
    k, n = w.shape
    w = f64(np.asarray(w, np.float32).astype(ml_dtypes.bfloat16)).reshape(k // 32, 32, n)
    amax = np.abs(w).max(1)
    byte = np.clip(np.where(amax > 0, np.frexp(amax)[1] - 1 + 127 - 7, 1), 1, 254)
    scaled = (w * np.exp2(127.0 - byte)[:, None, :]).reshape(k, n).astype(np.float32)
    words = np.ascontiguousarray(scaled.reshape(k // 512, 128, 4, n).transpose(0, 1, 3, 2)).astype(ml_dtypes.float8_e4m3fn).view(np.uint8)
    return words, np.ascontiguousarray(byte.astype(np.uint8).reshape(k // 512, 16, n))


def unpack_weight(words, scales):
    g, p, n, _ = words.shape
    vals = np.ascontiguousarray(words).view(ml_dtypes.float8_e4m3fn).astype(np.float64) * np.repeat(np.exp2(scales.astype(np.float64) - 127.0), 8, axis=1)[..., None]
    return vals.transpose(0, 1, 3, 2).reshape(g * 512, n)


K, T, S, H, G, U = 512, 1024, 256, 512, 2048, 512


def setup_inputs():
    n = np.random.standard_normal
    s = mx_kscale(K)[:, None]
    packed_xT = pack_weight(n((K, T)) * s)
    packed_w1 = pack_weight(n((K, H)) / np.sqrt(2 * K) / s)
    packed_w2 = pack_weight(n((K, H)) / np.sqrt(2 * K) / s)
    packed_dT = pack_weight(n((K, G)) / s)
    perm = np.random.permutation(U)
    return {
        "x_words": packed_xT[0],
        "x_scales": packed_xT[1],
        "w1_words": packed_w1[0],
        "w1_scales": packed_w1[1],
        "w2_words": packed_w2[0],
        "w2_scales": packed_w2[1],
        "gs": (np.random.uniform(0.5, 1.5, (K, 1)) * s).astype(np.float32),
        "d_words": packed_dT[0],
        "d_scales": packed_dT[1],
        "offs": striped8(np.random.randint(0, T, (8, S))),
        "hz": striped8(np.random.randint(0, T, (8, S))),
        "n1": striped(np.random.permutation(S)),
        "n2": striped(np.random.permutation(S)),
        "ka": striped8(np.random.randint(0, G, (8, H))),
        "kb": striped8(np.random.randint(0, G, (8, H))),
        "n3": striped(perm[:S]),
        "n4": striped(perm[S:]),
        "n5": striped(np.random.permutation(S)),
        "n6": striped(np.random.permutation(S)),
    }


def reference(x_words, x_scales, w1_words, w1_scales, w2_words, w2_scales, gs, d_words, d_scales, offs, hz, n1, n2, ka, kb, n3, n4, n5, n6):
    d_ka = unpack_weight(d_words, d_scales)[np.arange(K)[:, None], runs(ka, K)]
    xq = unpack_weight(x_words, x_scales)[np.arange(K)[:, None], runs(offs, K)]
    x_hz = unpack_weight(x_words, x_scales)[np.arange(K)[:, None], runs(hz, K)]
    y = unpack_weight(w1_words, w1_scales).T @ xq + unpack_weight(w2_words, w2_scales).T @ x_hz
    ds = np.zeros((H, S))
    ds[:, unstriped(n1)] = y
    z = f64(gs) * (np.maximum(y, ds[:, unstriped(n2)]))
    zq = mxq(z, 0, "e4m3")
    d_kb = unpack_weight(d_words, d_scales)[np.arange(K)[:, None], runs(kb, K)]
    h2 = 0.0625 * (d_ka.T @ zq + d_kb.T @ zq)
    st = h2 - h2[:, unstriped(n5)]
    up = np.maximum(st, st[:, unstriped(n6)])
    ph = np.zeros((H, U))
    ph[:, unstriped(n3)] = st
    out = ph.copy()
    out[:, unstriped(n4)] = up
    return out

@@ -1,0 +1,245 @@
+from contextlib import ExitStack
+
+import concourse.mybir as mybir
+
+K, T, S, H, G, U = 512, 1024, 256, 512, 2048, 512
+FLOPS = 2 * 2 * K * H * S + 2 * 2 * K * H * S
+
+F32 = mybir.dt.float32
+BF16 = mybir.dt.bfloat16
+I32 = mybir.dt.int32
+U32 = mybir.dt.uint32
+U16 = mybir.dt.uint16
+U8 = mybir.dt.uint8
+FP8X4 = mybir.dt.float8_e4m3fn_x4
+ALU = mybir.AluOpType
+COPY = mybir.ActivationFunctionType.Copy
+
+P = 128
+PACK = 4
+QUADS = 4
+DS_W = 384
+ROW_W = 272
+HALF = S // 2
+
+
+def tile_picked_dhhzarelaypagew_none_p_kernel(
+    tc, x_words, x_scales, w1_words, w1_scales, w2_words, w2_scales, gs, d_words, d_scales,
+    offs, hz, n1, n2, ka, kb, n3, n4, n5, n6, out,
+):
+    nc = tc.nc
+
+    with ExitStack() as ctx:
+        lists = ctx.enter_context(tc.tile_pool(name="lists", bufs=1))
+        keep = ctx.enter_context(tc.tile_pool(name="keep", bufs=1))
+        psum = ctx.enter_context(tc.psum_pool(name="psum", bufs=1))
+
+        def load_list(src, name):
+            tile = lists.tile(list(src.shape), U16, name=name)
+            nc.sync.dma_start(tile[:], src)
+            return tile
+
+        def words_view(words):
+            return words[0].rearrange("p n t -> p (n t)").bitcast(I32)
+
+        def load_scale_window(window, scales, queue):
+            for j in range(2):
+                queue.dma_start(window[j:P:16, :].bitcast(I32), scales[0][j:16:2, :].bitcast(I32))
+
+        def place_scale_rows(picked, plane, queue):
+            for j in range(2):
+                queue.dma_start(plane[2 + j : P : 32, :].bitcast(I32), picked[16 + j : P : 32, :].bitcast(I32))
+            for q in range(QUADS):
+                rows = slice(32 * q, 32 * q + 2)
+                nc.vector.tensor_copy(plane[rows, :].bitcast(I32), picked[rows, :].bitcast(I32))
+
+        offs_t = load_list(offs, "offs_t")
+        hz_t = load_list(hz, "hz_t")
+        xs_window = keep.tile([P, T], U8, name="xs_window", align_bytes=64)
+        for j in range(2):
+            rows = x_scales[0][j:16:2, :].bitcast(I32)
+            nc.sync.dma_start(xs_window[j:P:2, :].bitcast(I32), rows.unsqueeze(1).to_broadcast([8, 8, T // 4]))
+        ws_raw = keep.tile([P, H], U8, name="ws_raw", align_bytes=64)
+
+        def load_w_scales(a, j):
+            rows = (w1_scales, w2_scales)[a][0][j:16:4, :].bitcast(I32)
+            nc.sync.dma_start(
+                ws_raw[4 * a + j : P : 8, :].bitcast(I32), rows.unsqueeze(1).to_broadcast([4, 4, H // 4])
+            )
+
+        for j in range(3):
+            load_w_scales(0, j)
+        xw_window = keep.tile([P, T], I32, name="xw_window", tag="dw", align_bytes=64)
+        nc.sync.dma_start(xw_window[:], words_view(x_words))
+        load_w_scales(0, 3)
+        for j in range(4):
+            load_w_scales(1, j)
+        w_raw = []
+        for a, words in enumerate((w1_words, w2_words)):
+            raw = keep.tile([P, H], I32, name=f"w_raw{a}", tag=f"raw{a}", align_bytes=64)
+            nc.gpsimd.dma_start(raw[:], words_view(words))
+            w_raw.append(raw)
+        dsc_window = keep.tile([P, G], U8, name="dsc_window", tag="dsc", align_bytes=64)
+        nc.gpsimd.memset(dsc_window[:].bitcast(I32), 0)
+        load_scale_window(dsc_window, d_scales, nc.gpsimd)
+        xs_plane = keep.tile([P, 2 * S], U8, name="xs_plane", tag="xs_plane", align_bytes=64)
+        nc.vector.memset(xs_plane[:].bitcast(I32), 0)
+
+        xs_picked = keep.tile([P, 2 * S], U8, name="xs_picked", align_bytes=64)
+        for a, lst in enumerate((offs_t, hz_t)):
+            nc.vector.tensor_copy(xs_picked[:, a * S : (a + 1) * S], xs_window[:].indirect(lst[:]))
+        place_scale_rows(xs_picked, xs_plane, nc.scalar)
+        xw_picked = keep.tile([P, 2 * S], U32, name="xw_picked", align_bytes=64)
+        for a, lst in enumerate((offs_t, hz_t)):
+            nc.vector.tensor_copy(xw_picked[:, a * S : (a + 1) * S], xw_window[:].bitcast(U32).indirect(lst[:]))
+
+        ws_dealt = keep.tile([P, H], U8, name="ws_dealt", align_bytes=64)
+        nc.vector.tensor_copy(
+            ws_dealt[:].rearrange("p (t m) -> p m t", t=PACK), ws_raw[:].rearrange("p (m t) -> p m t", t=PACK)
+        )
+        w_dealt = []
+        for a in range(2):
+            dealt = keep.tile([P, H], U32, name=f"w_dealt{a}", tag=f"dealt{a}", align_bytes=64)
+            nc.scalar.copy(
+                dealt[:].rearrange("p (t m) -> p m t", t=PACK),
+                w_raw[a][:].bitcast(U32).rearrange("p (m t) -> p m t", t=PACK),
+            )
+            w_dealt.append(dealt)
+
+        dw_window = keep.tile([P, G], I32, name="dw_window", tag="dw", align_bytes=64)
+        nc.sync.dma_start(dw_window[:], words_view(d_words))
+        n1_t = load_list(n1, "n1_t")
+        n2_t = load_list(n2, "n2_t")
+        ka_t = load_list(ka, "ka_t")
+        kb_t = load_list(kb, "kb_t")
+        gs_t = keep.tile([P, PACK], F32, name="gs_t")
+        nc.gpsimd.dma_start(gs_t[:], gs.rearrange("(p t) o -> p (t o)", t=PACK))
+        n5_t = load_list(n5, "n5_t")
+        n6_t = load_list(n6, "n6_t")
+        n3_t = load_list(n3, "n3_t")
+        n4_t = load_list(n4, "n4_t")
+
+        ds_rows, h_rows, st_rows = [], [], []
+        for t in range(PACK):
+            ds_t = keep.tile([P, DS_W], F32, name=f"ds{t}")
+            nc.vector.memset(ds_t[:, S:], 0.0)
+            ds_rows.append(ds_t)
+        for t in range(PACK):
+            h_t = keep.tile([P, ROW_W], F32, name=f"h{t}")
+            nc.vector.memset(h_t[:, S:], 0.0)
+            h_rows.append(h_t)
+            st_t = keep.tile([P, ROW_W], F32, name=f"st{t}")
+            nc.vector.memset(st_t[:, S:], 0.0)
+            st_rows.append(st_t)
+
+        y_rows = []
+        for t in range(PACK):
+            cols = slice(t * P, (t + 1) * P)
+            acc = psum.tile([P, S], F32, name=f"y_acc{t}")
+            for a in range(2):
+                picked = slice(a * S, (a + 1) * S)
+                nc.tensor.matmul_mx(
+                    out=acc[:],
+                    lhsT=w_dealt[a][:, cols].bitcast(FP8X4),
+                    lhsT_scale=ws_dealt[4 * a : P, cols],
+                    rhs=xw_picked[:, picked].bitcast(FP8X4),
+                    rhs_scale=xs_plane[:, picked],
+                    start=(a == 0),
+                    stop=(a == 1),
+                )
+            y_t = keep.tile([P, S], F32, name=f"y{t}")
+            nc.vector.tensor_copy(y_t[:], acc[:])
+            y_rows.append(y_t)
+
+        dsc_plane = keep.tile([P, 2 * H], U8, name="dsc_plane", align_bytes=64)
+        nc.vector.memset(dsc_plane[:].bitcast(I32), 0)
+        dsc_picked = keep.tile([P, 2 * H], U8, name="dsc_picked", tag="xs_plane", align_bytes=64)
+        for a, lst in enumerate((ka_t, kb_t)):
+            nc.vector.tensor_copy(dsc_picked[:, a * H : (a + 1) * H], dsc_window[:].indirect(lst[:]))
+        place_scale_rows(dsc_picked, dsc_plane, nc.sync)
+        dw_picked = keep.tile([P, 2 * H], U32, name="dw_picked", align_bytes=64)
+        for a, lst in enumerate((ka_t, kb_t)):
+            nc.vector.tensor_copy(dw_picked[:, a * H : (a + 1) * H], dw_window[:].bitcast(U32).indirect(lst[:]))
+
+        fetched = [
+            keep.tile([P, S], F32, name=f"ds_fetched{t}", tag=f"dealt{t}", align_bytes=64) for t in range(PACK)
+        ]
+        larger = keep.tile([P, PACK, S], F32, name="larger", tag="dsc", align_bytes=64)
+        z = keep.tile([P, S, PACK], BF16, name="z", tag="dw", align_bytes=64)
+        z_words = keep.tile([P, S], U32, name="z_words", align_bytes=64)
+        z_plane = keep.tile([P, S], U8, name="z_plane", align_bytes=64)
+
+        def scatter_y(t):
+            nc.scalar.activation(ds_rows[t][:].indirect(n1_t[:]), y_rows[t][:], COPY)
+
+        def make_z(t, lo, hi):
+            nc.scalar.activation(fetched[t][:, lo:hi], ds_rows[t][:].indirect(n2_t[:, lo // 16 : hi // 16]), COPY)
+            nc.vector.tensor_tensor(larger[:, t, lo:hi], y_rows[t][:, lo:hi], fetched[t][:, lo:hi], ALU.max)
+            nc.vector.tensor_scalar(z[:, lo:hi, t], larger[:, t, lo:hi], gs_t[:, t : t + 1], None, ALU.mult)
+
+        def quantize_z(lo, hi):
+            nc.vector.quantize_mx(
+                out=z_words[:, lo:hi].bitcast(FP8X4),
+                scales=z_plane[:, lo:hi],
+                in_=z[:, lo:hi, :].rearrange("p j t -> p (j t)"),
+            )
+
+        scatter_y(0)
+        scatter_y(1)
+        make_z(0, 0, S)
+        scatter_y(2)
+        make_z(1, 0, S)
+        make_z(2, 0, S)
+        scatter_y(3)
+        make_z(3, 0, HALF)
+        make_z(3, HALF, S)
+        quantize_z(0, HALF)
+        quantize_z(HALF, S)
+
+        h_acc = [psum.tile([P, S], F32, name=f"h_acc{t}") for t in range(PACK)]
+        for t in range(PACK):
+            for lo, hi in ((0, HALF), (HALF, S)) if t == 0 else ((0, S),):
+                for a in range(2):
+                    cols = slice(a * H + t * P, a * H + (t + 1) * P)
+                    nc.tensor.matmul_mx(
+                        out=h_acc[t][:, lo:hi],
+                        lhsT=dw_picked[:, cols].bitcast(FP8X4),
+                        lhsT_scale=dsc_plane[:, cols],
+                        rhs=z_words[:, lo:hi].bitcast(FP8X4),
+                        rhs_scale=z_plane[:, lo:hi],
+                        start=(a == 0),
+                        stop=(a == 1),
+                    )
+
+        h_fetched = [keep.tile([P, S], F32, name=f"h_fetched{t}") for t in range(PACK)]
+        st_fetched = [keep.tile([P, S], F32, name=f"st_fetched{t}") for t in range(PACK)]
+        up_rows = [keep.tile([P, S], F32, name=f"up{t}") for t in range(PACK)]
+        pages = [keep.tile([P, U], F32, name=f"page{t}") for t in range(PACK)]
+
+        for t in range(PACK):
+            nc.vector.tensor_scalar(h_rows[t][:, :S], h_acc[t][:], 0.0625, None, ALU.mult)
+
+        def make_st(t):
+            nc.scalar.activation(h_fetched[t][:], h_rows[t][:].indirect(n5_t[:]), COPY)
+            nc.vector.tensor_tensor(st_rows[t][:, :S], h_rows[t][:, :S], h_fetched[t][:], ALU.subtract)
+
+        def make_up(t):
+            nc.scalar.activation(st_fetched[t][:], st_rows[t][:].indirect(n6_t[:]), COPY)
+            nc.vector.tensor_tensor(up_rows[t][:], st_rows[t][:, :S], st_fetched[t][:], ALU.max)
+
+        def put_st(t):
+            nc.scalar.activation(pages[t][:].indirect(n3_t[:]), st_rows[t][:, :S], COPY)
+
+        def put_up(t):
+            nc.scalar.activation(pages[t][:].indirect(n4_t[:]), up_rows[t][:], COPY)
+            nc.sync.dma_start(out[t * P : (t + 1) * P, :], pages[t][:])
+
+        make_st(0)
+        for t in range(PACK):
+            if t + 1 < PACK:
+                make_st(t + 1)
+            make_up(t)
+            put_st(t)
+            if t > 0:
+                put_up(t - 1)
+        put_up(PACK - 1)

@@ -42,9 +42,17 @@ def tile_picked_dhhzarelaypagew_none_p_kernel(
         def words_view(words):
             return words[0].rearrange("p n t -> p (n t)").bitcast(I32)
 
-        def load_scale_window(window, scales, queue):
+        def load_scale_window(scales, width, name, tag):
+            window = keep.tile([P, width], U8, name=name, tag=tag, align_bytes=64)
             for j in range(2):
-                queue.dma_start(window[j:P:16, :].bitcast(I32), scales[0][j:16:2, :].bitcast(I32))
+                rows = scales[0][j:16:2, :].bitcast(I32)
+                nc.sync.dma_start(window[j:P:2, :].bitcast(I32), rows.unsqueeze(1).to_broadcast([8, 8, width // 4]))
+            return window
+
+        def move_scale_rows(picked, plane):
+            for j in range(4):
+                first = 16 * (j // 2) + j % 2
+                nc.sync.dma_start(plane[j:P:32, :].bitcast(I32), picked[first:P:32, :].bitcast(I32))
 
         def place_scale_rows(picked, plane, queue):
             for j in range(2):
@@ -55,10 +63,7 @@ def tile_picked_dhhzarelaypagew_none_p_kernel(
 
         offs_t = load_list(offs, "offs_t")
         hz_t = load_list(hz, "hz_t")
-        xs_window = keep.tile([P, T], U8, name="xs_window", align_bytes=64)
-        for j in range(2):
-            rows = x_scales[0][j:16:2, :].bitcast(I32)
-            nc.sync.dma_start(xs_window[j:P:2, :].bitcast(I32), rows.unsqueeze(1).to_broadcast([8, 8, T // 4]))
+        xs_window = load_scale_window(x_scales, T, "xs_window", "xs_window")
         ws_raw = keep.tile([P, H], U8, name="ws_raw", align_bytes=64)
 
         def load_w_scales(a, j):
@@ -79,17 +84,14 @@ def tile_picked_dhhzarelaypagew_none_p_kernel(
             raw = keep.tile([P, H], I32, name=f"w_raw{a}", tag=f"raw{a}", align_bytes=64)
             nc.gpsimd.dma_start(raw[:], words_view(words))
             w_raw.append(raw)
-        dsc_window = keep.tile([P, G], U8, name="dsc_window", tag="dsc", align_bytes=64)
-        nc.gpsimd.memset(dsc_window[:].bitcast(I32), 0)
-        load_scale_window(dsc_window, d_scales, nc.gpsimd)
         xs_plane = keep.tile([P, 2 * S], U8, name="xs_plane", tag="xs_plane", align_bytes=64)
         nc.vector.memset(xs_plane[:].bitcast(I32), 0)
 
         xs_picked = keep.tile([P, 2 * S], U8, name="xs_picked", align_bytes=64)
         for a, lst in enumerate((offs_t, hz_t)):
             nc.vector.tensor_copy(xs_picked[:, a * S : (a + 1) * S], xs_window[:].indirect(lst[:]))
-        place_scale_rows(xs_picked, xs_plane, nc.scalar)
-        xw_picked = keep.tile([P, 2 * S], U32, name="xw_picked", align_bytes=64)
+        place_scale_rows(xs_picked, xs_plane, nc.sync)
+        xw_picked = keep.tile([P, 2 * S], U32, name="xw_picked", tag="picked", align_bytes=64)
         for a, lst in enumerate((offs_t, hz_t)):
             nc.vector.tensor_copy(xw_picked[:, a * S : (a + 1) * S], xw_window[:].bitcast(U32).indirect(lst[:]))
 
@@ -106,12 +108,13 @@ def tile_picked_dhhzarelaypagew_none_p_kernel(
             )
             w_dealt.append(dealt)
 
-        dw_window = keep.tile([P, G], I32, name="dw_window", tag="dw", align_bytes=64)
-        nc.sync.dma_start(dw_window[:], words_view(d_words))
         n1_t = load_list(n1, "n1_t")
         n2_t = load_list(n2, "n2_t")
         ka_t = load_list(ka, "ka_t")
         kb_t = load_list(kb, "kb_t")
+        dw_window = keep.tile([P, G], I32, name="dw_window", tag="dw", align_bytes=64)
+        nc.sync.dma_start(dw_window[:], words_view(d_words))
+        dsc_window = load_scale_window(d_scales, G, "dsc_window", "raw1")
         gs_t = keep.tile([P, PACK], F32, name="gs_t")
         nc.gpsimd.dma_start(gs_t[:], gs.rearrange("(p t) o -> p (t o)", t=PACK))
         n5_t = load_list(n5, "n5_t")
@@ -136,7 +139,7 @@ def tile_picked_dhhzarelaypagew_none_p_kernel(
         for t in range(PACK):
             cols = slice(t * P, (t + 1) * P)
             acc = psum.tile([P, S], F32, name=f"y_acc{t}")
-            for a in range(2):
+            for a in (1, 0):
                 picked = slice(a * S, (a + 1) * S)
                 nc.tensor.matmul_mx(
                     out=acc[:],
@@ -144,28 +147,33 @@ def tile_picked_dhhzarelaypagew_none_p_kernel(
                     lhsT_scale=ws_dealt[4 * a : P, cols],
                     rhs=xw_picked[:, picked].bitcast(FP8X4),
                     rhs_scale=xs_plane[:, picked],
-                    start=(a == 0),
-                    stop=(a == 1),
+                    start=(a == 1),
+                    stop=(a == 0),
                 )
             y_t = keep.tile([P, S], F32, name=f"y{t}")
             nc.vector.tensor_copy(y_t[:], acc[:])
             y_rows.append(y_t)
 
+        def pick_d_words(pair, tag):
+            picked = keep.tile([P, 2, 2 * P], U32, name=f"dw_picked{pair}", tag=tag, align_bytes=64)
+            entries = slice(pair * 2 * P // 16, (pair + 1) * 2 * P // 16)
+            for a, lst in enumerate((ka_t, kb_t)):
+                nc.vector.tensor_copy(picked[:, a, :], dw_window[:].bitcast(U32).indirect(lst[:, entries]))
+            return picked
+
+        dw_first = pick_d_words(0, "picked")
         dsc_plane = keep.tile([P, 2 * H], U8, name="dsc_plane", align_bytes=64)
         nc.vector.memset(dsc_plane[:].bitcast(I32), 0)
         dsc_picked = keep.tile([P, 2 * H], U8, name="dsc_picked", tag="xs_plane", align_bytes=64)
         for a, lst in enumerate((ka_t, kb_t)):
             nc.vector.tensor_copy(dsc_picked[:, a * H : (a + 1) * H], dsc_window[:].indirect(lst[:]))
-        place_scale_rows(dsc_picked, dsc_plane, nc.sync)
-        dw_picked = keep.tile([P, 2 * H], U32, name="dw_picked", align_bytes=64)
-        for a, lst in enumerate((ka_t, kb_t)):
-            nc.vector.tensor_copy(dw_picked[:, a * H : (a + 1) * H], dw_window[:].bitcast(U32).indirect(lst[:]))
+        move_scale_rows(dsc_picked, dsc_plane)
 
         fetched = [
             keep.tile([P, S], F32, name=f"ds_fetched{t}", tag=f"dealt{t}", align_bytes=64) for t in range(PACK)
         ]
-        larger = keep.tile([P, PACK, S], F32, name="larger", tag="dsc", align_bytes=64)
-        z = keep.tile([P, S, PACK], BF16, name="z", tag="dw", align_bytes=64)
+        larger = keep.tile([P, PACK, S], F32, name="larger", tag="raw1", align_bytes=64)
+        z = keep.tile([P, S, PACK], BF16, name="z", align_bytes=64)
         z_words = keep.tile([P, S], U32, name="z_words", align_bytes=64)
         z_plane = keep.tile([P, S], U8, name="z_plane", align_bytes=64)
 
@@ -196,28 +204,27 @@ def tile_picked_dhhzarelaypagew_none_p_kernel(
         quantize_z(0, HALF)
         quantize_z(HALF, S)
 
-        h_acc = [psum.tile([P, S], F32, name=f"h_acc{t}") for t in range(PACK)]
-        for t in range(PACK):
-            for lo, hi in ((0, HALF), (HALF, S)) if t == 0 else ((0, S),):
+        def second_product(t, picked, pieces):
+            acc = psum.tile([P, S], F32, name=f"h_acc{t}")
+            for lo, hi in pieces:
                 for a in range(2):
-                    cols = slice(a * H + t * P, a * H + (t + 1) * P)
                     nc.tensor.matmul_mx(
-                        out=h_acc[t][:, lo:hi],
-                        lhsT=dw_picked[:, cols].bitcast(FP8X4),
-                        lhsT_scale=dsc_plane[:, cols],
+                        out=acc[:, lo:hi],
+                        lhsT=picked[:, a, (t % 2) * P : (t % 2 + 1) * P].bitcast(FP8X4),
+                        lhsT_scale=dsc_plane[:, a * H + t * P : a * H + (t + 1) * P],
                         rhs=z_words[:, lo:hi].bitcast(FP8X4),
                         rhs_scale=z_plane[:, lo:hi],
                         start=(a == 0),
                         stop=(a == 1),
                     )
+            nc.vector.tensor_scalar(h_rows[t][:, :S], acc[:], 0.0625, None, ALU.mult)
 
-        h_fetched = [keep.tile([P, S], F32, name=f"h_fetched{t}") for t in range(PACK)]
+        h_fetched = [
+            keep.tile([P, S], F32, name=f"h_fetched{t}", tag=f"h_fetched{t}", align_bytes=64) for t in range(PACK)
+        ]
         st_fetched = [keep.tile([P, S], F32, name=f"st_fetched{t}") for t in range(PACK)]
         up_rows = [keep.tile([P, S], F32, name=f"up{t}") for t in range(PACK)]
         pages = [keep.tile([P, U], F32, name=f"page{t}") for t in range(PACK)]
-
-        for t in range(PACK):
-            nc.vector.tensor_scalar(h_rows[t][:, :S], h_acc[t][:], 0.0625, None, ALU.mult)
 
         def make_st(t):
             nc.scalar.activation(h_fetched[t][:], h_rows[t][:].indirect(n5_t[:]), COPY)
@@ -234,12 +241,21 @@ def tile_picked_dhhzarelaypagew_none_p_kernel(
             nc.scalar.activation(pages[t][:].indirect(n4_t[:]), up_rows[t][:], COPY)
             nc.sync.dma_start(out[t * P : (t + 1) * P, :], pages[t][:])
 
+        def finish_pair(first):
+            for t in (first, first + 1):
+                make_up(t)
+                put_st(t)
+            for t in (first, first + 1):
+                put_up(t)
+
+        second_product(0, dw_first, ((0, HALF), (HALF, S)))
+        second_product(1, dw_first, ((0, S),))
         make_st(0)
-        for t in range(PACK):
-            if t + 1 < PACK:
-                make_st(t + 1)
-            make_up(t)
-            put_st(t)
-            if t > 0:
-                put_up(t - 1)
-        put_up(PACK - 1)
+        make_st(1)
+        dw_second = pick_d_words(1, "h_fetched0")
+        second_product(2, dw_second, ((0, S),))
+        second_product(3, dw_second, ((0, S),))
+        finish_pair(0)
+        make_st(2)
+        make_st(3)
+        finish_pair(2)

@@ -54,13 +54,6 @@ def tile_picked_dhhzarelaypagew_none_p_kernel(
                 first = 16 * (j // 2) + j % 2
                 nc.sync.dma_start(plane[j:P:32, :].bitcast(I32), picked[first:P:32, :].bitcast(I32))
 
-        def place_scale_rows(picked, plane, queue):
-            for j in range(2):
-                queue.dma_start(plane[2 + j : P : 32, :].bitcast(I32), picked[16 + j : P : 32, :].bitcast(I32))
-            for q in range(QUADS):
-                rows = slice(32 * q, 32 * q + 2)
-                nc.vector.tensor_copy(plane[rows, :].bitcast(I32), picked[rows, :].bitcast(I32))
-
         offs_t = load_list(offs, "offs_t")
         hz_t = load_list(hz, "hz_t")
         xs_window = load_scale_window(x_scales, T, "xs_window", "xs_window")
@@ -84,28 +77,56 @@ def tile_picked_dhhzarelaypagew_none_p_kernel(
             raw = keep.tile([P, H], I32, name=f"w_raw{a}", tag=f"raw{a}", align_bytes=64)
             nc.gpsimd.dma_start(raw[:], words_view(words))
             w_raw.append(raw)
-        xs_plane = keep.tile([P, 2 * S], U8, name="xs_plane", tag="xs_plane", align_bytes=64)
-        nc.vector.memset(xs_plane[:].bitcast(I32), 0)
+        xs_plane = keep.tile([P, 2, 2 * HALF], U8, name="xs_plane", tag="xs_plane", align_bytes=64)
+        nc.vector.memset(xs_plane[:].rearrange("p a s -> p (a s)").bitcast(I32), 0)
 
-        xs_picked = keep.tile([P, 2 * S], U8, name="xs_picked", align_bytes=64)
-        for a, lst in enumerate((offs_t, hz_t)):
-            nc.vector.tensor_copy(xs_picked[:, a * S : (a + 1) * S], xs_window[:].indirect(lst[:]))
-        place_scale_rows(xs_picked, xs_plane, nc.sync)
-        xw_picked = keep.tile([P, 2 * S], U32, name="xw_picked", tag="picked", align_bytes=64)
-        for a, lst in enumerate((offs_t, hz_t)):
-            nc.vector.tensor_copy(xw_picked[:, a * S : (a + 1) * S], xw_window[:].bitcast(U32).indirect(lst[:]))
+        halves = (slice(0, HALF), slice(HALF, S))
+        xs_picked = keep.tile([P, 2, 2 * HALF], U8, name="xs_picked", align_bytes=64)
+        xw_picked = keep.tile([P, 2, 2 * HALF], U32, name="xw_picked", tag="picked", align_bytes=64)
 
+        def entries(cols):
+            return slice(cols.start // 16, cols.stop // 16)
+
+        for h in range(2):
+            for a, lst in enumerate((offs_t, hz_t)):
+                nc.vector.tensor_copy(xs_picked[:, h, halves[a]], xs_window[:].indirect(lst[:, entries(halves[h])]))
+            for j in range(2):
+                nc.sync.dma_start(
+                    xs_plane[2 + j : P : 32, h, :].bitcast(I32), xs_picked[16 + j : P : 32, h, :].bitcast(I32)
+                )
+        for q in range(QUADS):
+            rows = slice(32 * q, 32 * q + 2)
+            nc.vector.tensor_copy(
+                xs_plane[rows, :, :].rearrange("p h s -> p (h s)").bitcast(I32),
+                xs_picked[rows, :, :].rearrange("p h s -> p (h s)").bitcast(I32),
+            )
+
+        def pick_x_words(h):
+            for a, lst in enumerate((offs_t, hz_t)):
+                nc.vector.tensor_copy(
+                    xw_picked[:, h, halves[a]], xw_window[:].bitcast(U32).indirect(lst[:, entries(halves[h])])
+                )
+
+        pick_x_words(0)
         ws_dealt = keep.tile([P, H], U8, name="ws_dealt", align_bytes=64)
-        nc.vector.tensor_copy(
-            ws_dealt[:].rearrange("p (t m) -> p m t", t=PACK), ws_raw[:].rearrange("p (m t) -> p m t", t=PACK)
-        )
+
+        def deal_w_scales(tiles):
+            nc.vector.tensor_copy(
+                ws_dealt[:].rearrange("p (t m) -> p m t", t=PACK)[:, :, tiles],
+                ws_raw[:].rearrange("p (m t) -> p m t", t=PACK)[:, :, tiles],
+            )
+
+        deal_w_scales(slice(0, 2))
+        pick_x_words(1)
+        deal_w_scales(slice(2, 4))
         w_dealt = []
         for a in range(2):
             dealt = keep.tile([P, H], U32, name=f"w_dealt{a}", tag=f"dealt{a}", align_bytes=64)
-            nc.scalar.copy(
-                dealt[:].rearrange("p (t m) -> p m t", t=PACK),
-                w_raw[a][:].bitcast(U32).rearrange("p (m t) -> p m t", t=PACK),
-            )
+            for tiles in (slice(0, 2), slice(2, 4)):
+                nc.scalar.copy(
+                    dealt[:].rearrange("p (t m) -> p m t", t=PACK)[:, :, tiles],
+                    w_raw[a][:].bitcast(U32).rearrange("p (m t) -> p m t", t=PACK)[:, :, tiles],
+                )
             w_dealt.append(dealt)
 
         n1_t = load_list(n1, "n1_t")
@@ -116,7 +137,7 @@ def tile_picked_dhhzarelaypagew_none_p_kernel(
         nc.sync.dma_start(dw_window[:], words_view(d_words))
         dsc_window = load_scale_window(d_scales, G, "dsc_window", "raw1")
         gs_t = keep.tile([P, PACK], F32, name="gs_t")
-        nc.gpsimd.dma_start(gs_t[:], gs.rearrange("(p t) o -> p (t o)", t=PACK))
+        nc.sync.dma_start(gs_t[:], gs.rearrange("(p t) o -> p (t o)", t=PACK))
         n5_t = load_list(n5, "n5_t")
         n6_t = load_list(n6, "n6_t")
         n3_t = load_list(n3, "n3_t")
@@ -135,30 +156,31 @@ def tile_picked_dhhzarelaypagew_none_p_kernel(
             nc.vector.memset(st_t[:, S:], 0.0)
             st_rows.append(st_t)
 
-        y_rows = []
-        for t in range(PACK):
-            cols = slice(t * P, (t + 1) * P)
-            acc = psum.tile([P, S], F32, name=f"y_acc{t}")
-            for a in (1, 0):
-                picked = slice(a * S, (a + 1) * S)
-                nc.tensor.matmul_mx(
-                    out=acc[:],
-                    lhsT=w_dealt[a][:, cols].bitcast(FP8X4),
-                    lhsT_scale=ws_dealt[4 * a : P, cols],
-                    rhs=xw_picked[:, picked].bitcast(FP8X4),
-                    rhs_scale=xs_plane[:, picked],
-                    start=(a == 1),
-                    stop=(a == 0),
-                )
-            y_t = keep.tile([P, S], F32, name=f"y{t}")
-            nc.vector.tensor_copy(y_t[:], acc[:])
-            y_rows.append(y_t)
+        y_rows = [keep.tile([P, S], F32, name=f"y{t}") for t in range(PACK)]
+        whole = slice(0, S)
+        y_pieces = [(t, cols) for cols in halves for t in (0, 1)] + [(2, whole), (3, whole)]
+        for bank, (t, cols) in enumerate(y_pieces):
+            rows = slice(t * P, (t + 1) * P)
+            acc = psum.tile([P, cols.stop - cols.start], F32, name=f"y_acc{bank}", tag=f"bank{bank}")
+            for h in range(cols.start // HALF, cols.stop // HALF):
+                lo = h * HALF - cols.start
+                for a in (1, 0):
+                    nc.tensor.matmul_mx(
+                        out=acc[:, lo : lo + HALF],
+                        lhsT=w_dealt[a][:, rows].bitcast(FP8X4),
+                        lhsT_scale=ws_dealt[4 * a : P, rows],
+                        rhs=xw_picked[:, h, halves[a]].bitcast(FP8X4),
+                        rhs_scale=xs_plane[:, h, halves[a]],
+                        start=(a == 1),
+                        stop=(a == 0),
+                    )
+            nc.vector.tensor_copy(y_rows[t][:, cols], acc[:])
 
         def pick_d_words(pair, tag):
             picked = keep.tile([P, 2, 2 * P], U32, name=f"dw_picked{pair}", tag=tag, align_bytes=64)
-            entries = slice(pair * 2 * P // 16, (pair + 1) * 2 * P // 16)
+            rows = slice(pair * 2 * P, (pair + 1) * 2 * P)
             for a, lst in enumerate((ka_t, kb_t)):
-                nc.vector.tensor_copy(picked[:, a, :], dw_window[:].bitcast(U32).indirect(lst[:, entries]))
+                nc.vector.tensor_copy(picked[:, a, :], dw_window[:].bitcast(U32).indirect(lst[:, entries(rows)]))
             return picked
 
         dw_first = pick_d_words(0, "picked")
@@ -177,8 +199,8 @@ def tile_picked_dhhzarelaypagew_none_p_kernel(
         z_words = keep.tile([P, S], U32, name="z_words", align_bytes=64)
         z_plane = keep.tile([P, S], U8, name="z_plane", align_bytes=64)
 
-        def scatter_y(t):
-            nc.scalar.activation(ds_rows[t][:].indirect(n1_t[:]), y_rows[t][:], COPY)
+        def scatter_y(t, cols):
+            nc.scalar.activation(ds_rows[t][:].indirect(n1_t[:, entries(cols)]), y_rows[t][:, cols], COPY)
 
         def make_z(t, lo, hi):
             nc.scalar.activation(fetched[t][:, lo:hi], ds_rows[t][:].indirect(n2_t[:, lo // 16 : hi // 16]), COPY)
@@ -192,24 +214,22 @@ def tile_picked_dhhzarelaypagew_none_p_kernel(
                 in_=z[:, lo:hi, :].rearrange("p j t -> p (j t)"),
             )
 
-        scatter_y(0)
-        scatter_y(1)
-        make_z(0, 0, S)
-        scatter_y(2)
-        make_z(1, 0, S)
-        make_z(2, 0, S)
-        scatter_y(3)
+        for t, cols in y_pieces[:5]:
+            scatter_y(t, cols)
+        for t in range(3):
+            make_z(t, 0, S)
+        scatter_y(3, whole)
         make_z(3, 0, HALF)
         make_z(3, HALF, S)
         quantize_z(0, HALF)
         quantize_z(HALF, S)
 
         def second_product(t, picked, pieces):
-            acc = psum.tile([P, S], F32, name=f"h_acc{t}")
-            for lo, hi in pieces:
+            for lo, hi, bank in pieces:
+                acc = psum.tile([P, hi - lo], F32, name=f"h_acc{bank}", tag=f"bank{bank}")
                 for a in range(2):
                     nc.tensor.matmul_mx(
-                        out=acc[:, lo:hi],
+                        out=acc[:],
                         lhsT=picked[:, a, (t % 2) * P : (t % 2 + 1) * P].bitcast(FP8X4),
                         lhsT_scale=dsc_plane[:, a * H + t * P : a * H + (t + 1) * P],
                         rhs=z_words[:, lo:hi].bitcast(FP8X4),
@@ -217,13 +237,12 @@ def tile_picked_dhhzarelaypagew_none_p_kernel(
                         start=(a == 0),
                         stop=(a == 1),
                     )
-            nc.vector.tensor_scalar(h_rows[t][:, :S], acc[:], 0.0625, None, ALU.mult)
+                nc.vector.tensor_scalar(h_rows[t][:, lo:hi], acc[:], 0.0625, None, ALU.mult)
 
         h_fetched = [
             keep.tile([P, S], F32, name=f"h_fetched{t}", tag=f"h_fetched{t}", align_bytes=64) for t in range(PACK)
         ]
         st_fetched = [keep.tile([P, S], F32, name=f"st_fetched{t}") for t in range(PACK)]
-        up_rows = [keep.tile([P, S], F32, name=f"up{t}") for t in range(PACK)]
         pages = [keep.tile([P, U], F32, name=f"page{t}") for t in range(PACK)]
 
         def make_st(t):
@@ -232,30 +251,34 @@ def tile_picked_dhhzarelaypagew_none_p_kernel(
 
         def make_up(t):
             nc.scalar.activation(st_fetched[t][:], st_rows[t][:].indirect(n6_t[:]), COPY)
-            nc.vector.tensor_tensor(up_rows[t][:], st_rows[t][:, :S], st_fetched[t][:], ALU.max)
+            nc.vector.tensor_tensor(up_rows[t], st_rows[t][:, :S], st_fetched[t][:], ALU.max)
 
         def put_st(t):
             nc.scalar.activation(pages[t][:].indirect(n3_t[:]), st_rows[t][:, :S], COPY)
 
         def put_up(t):
-            nc.scalar.activation(pages[t][:].indirect(n4_t[:]), up_rows[t][:], COPY)
+            nc.scalar.activation(pages[t][:].indirect(n4_t[:]), up_rows[t], COPY)
             nc.sync.dma_start(out[t * P : (t + 1) * P, :], pages[t][:])
 
-        def finish_pair(first):
-            for t in (first, first + 1):
-                make_up(t)
-                put_st(t)
-            for t in (first, first + 1):
-                put_up(t)
-
-        second_product(0, dw_first, ((0, HALF), (HALF, S)))
-        second_product(1, dw_first, ((0, S),))
+        second_product(0, dw_first, ((0, HALF, 0), (HALF, S, 1)))
+        second_product(1, dw_first, ((0, S, 2),))
         make_st(0)
         make_st(1)
         dw_second = pick_d_words(1, "h_fetched0")
-        second_product(2, dw_second, ((0, S),))
-        second_product(3, dw_second, ((0, S),))
-        finish_pair(0)
+        second_product(2, dw_second, ((0, S, 3),))
+        second_product(3, dw_second, ((0, S, 4),))
+        up_first = keep.tile([P, 2, S], F32, name="up_first", tag="h_fetched0", align_bytes=64)
+        up_second = keep.tile([P, 2, S], F32, name="up_second")
+        up_rows = [up_first[:, 0, :], up_first[:, 1, :], up_second[:, 0, :], up_second[:, 1, :]]
+        for t in (0, 1):
+            make_up(t)
+            put_st(t)
         make_st(2)
         make_st(3)
-        finish_pair(2)
+        put_up(0)
+        put_up(1)
+        for t in (2, 3):
+            make_up(t)
+            put_st(t)
+        put_up(2)
+        put_up(3)

@@ -18,9 +18,13 @@ COPY = mybir.ActivationFunctionType.Copy
 P = 128
 PACK = 4
 QUADS = 4
-DS_W = 384
-ROW_W = 272
+BLOCKS = 16
 HALF = S // 2
+MX_ALIGN = 64
+DS_WIDTH = S + HALF
+ROW_WIDTH = S + 16
+W_SCALES_FIRST = 1
+H2_FACTOR = 0.0625
 
 
 def tile_picked_dhhzarelaypagew_none_p_kernel(
@@ -28,6 +32,9 @@ def tile_picked_dhhzarelaypagew_none_p_kernel(
     offs, hz, n1, n2, ka, kb, n3, n4, n5, n6, out,
 ):
     nc = tc.nc
+    halves = (slice(0, HALF), slice(HALF, S))
+    whole = slice(0, S)
+    tile_pairs = (slice(0, 2), slice(2, 4))
 
     with ExitStack() as ctx:
         lists = ctx.enter_context(tc.tile_pool(name="lists", bufs=1))
@@ -39,53 +46,48 @@ def tile_picked_dhhzarelaypagew_none_p_kernel(
             nc.sync.dma_start(tile[:], src)
             return tile
 
+        def entries(span):
+            return slice(span.start // 16, span.stop // 16)
+
         def words_view(words):
             return words[0].rearrange("p n t -> p (n t)").bitcast(I32)
 
         def load_scale_window(scales, width, name, tag):
-            window = keep.tile([P, width], U8, name=name, tag=tag, align_bytes=64)
+            window = keep.tile([P, width], U8, name=name, tag=tag, align_bytes=MX_ALIGN)
             for j in range(2):
-                rows = scales[0][j:16:2, :].bitcast(I32)
+                rows = scales[0][j:BLOCKS:2, :].bitcast(I32)
                 nc.sync.dma_start(window[j:P:2, :].bitcast(I32), rows.unsqueeze(1).to_broadcast([8, 8, width // 4]))
             return window
-
-        def move_scale_rows(picked, plane):
-            for j in range(4):
-                first = 16 * (j // 2) + j % 2
-                nc.sync.dma_start(plane[j:P:32, :].bitcast(I32), picked[first:P:32, :].bitcast(I32))
 
         offs_t = load_list(offs, "offs_t")
         hz_t = load_list(hz, "hz_t")
         xs_window = load_scale_window(x_scales, T, "xs_window", "xs_window")
-        ws_raw = keep.tile([P, H], U8, name="ws_raw", align_bytes=64)
+
+        ws_raw = keep.tile([P, H], U8, name="ws_raw", align_bytes=MX_ALIGN)
 
         def load_w_scales(a, j):
-            rows = (w1_scales, w2_scales)[a][0][j:16:4, :].bitcast(I32)
+            rows = (w1_scales, w2_scales)[a][0][j:BLOCKS:4, :].bitcast(I32)
             nc.sync.dma_start(
                 ws_raw[4 * a + j : P : 8, :].bitcast(I32), rows.unsqueeze(1).to_broadcast([4, 4, H // 4])
             )
 
-        for j in range(3):
-            load_w_scales(0, j)
-        xw_window = keep.tile([P, T], I32, name="xw_window", tag="dw", align_bytes=64)
+        w_scale_loads = [(a, j) for a in range(2) for j in range(4)]
+        for a, j in w_scale_loads[:W_SCALES_FIRST]:
+            load_w_scales(a, j)
+        xw_window = keep.tile([P, T], I32, name="xw_window", tag="dw", align_bytes=MX_ALIGN)
         nc.sync.dma_start(xw_window[:], words_view(x_words))
-        load_w_scales(0, 3)
-        for j in range(4):
-            load_w_scales(1, j)
+        for a, j in w_scale_loads[W_SCALES_FIRST:]:
+            load_w_scales(a, j)
         w_raw = []
         for a, words in enumerate((w1_words, w2_words)):
-            raw = keep.tile([P, H], I32, name=f"w_raw{a}", tag=f"raw{a}", align_bytes=64)
+            raw = keep.tile([P, H], I32, name=f"w_raw{a}", tag=f"raw{a}", align_bytes=MX_ALIGN)
             nc.gpsimd.dma_start(raw[:], words_view(words))
             w_raw.append(raw)
-        xs_plane = keep.tile([P, 2, 2 * HALF], U8, name="xs_plane", tag="xs_plane", align_bytes=64)
-        nc.vector.memset(xs_plane[:].rearrange("p a s -> p (a s)").bitcast(I32), 0)
 
-        halves = (slice(0, HALF), slice(HALF, S))
-        xs_picked = keep.tile([P, 2, 2 * HALF], U8, name="xs_picked", align_bytes=64)
-        xw_picked = keep.tile([P, 2, 2 * HALF], U32, name="xw_picked", tag="picked", align_bytes=64)
-
-        def entries(cols):
-            return slice(cols.start // 16, cols.stop // 16)
+        xs_plane = keep.tile([P, 2, 2 * HALF], U8, name="xs_plane", tag="xs_plane", align_bytes=MX_ALIGN)
+        nc.vector.memset(xs_plane[:].rearrange("p h s -> p (h s)").bitcast(I32), 0)
+        xs_picked = keep.tile([P, 2, 2 * HALF], U8, name="xs_picked", align_bytes=MX_ALIGN)
+        xw_picked = keep.tile([P, 2, 2 * HALF], U32, name="xw_picked", tag="picked", align_bytes=MX_ALIGN)
 
         for h in range(2):
             for a, lst in enumerate((offs_t, hz_t)):
@@ -95,10 +97,10 @@ def tile_picked_dhhzarelaypagew_none_p_kernel(
                     xs_plane[2 + j : P : 32, h, :].bitcast(I32), xs_picked[16 + j : P : 32, h, :].bitcast(I32)
                 )
         for q in range(QUADS):
-            rows = slice(32 * q, 32 * q + 2)
+            even_rows = slice(32 * q, 32 * q + 2)
             nc.vector.tensor_copy(
-                xs_plane[rows, :, :].rearrange("p h s -> p (h s)").bitcast(I32),
-                xs_picked[rows, :, :].rearrange("p h s -> p (h s)").bitcast(I32),
+                xs_plane[even_rows, :, :].rearrange("p h s -> p (h s)").bitcast(I32),
+                xs_picked[even_rows, :, :].rearrange("p h s -> p (h s)").bitcast(I32),
             )
 
         def pick_x_words(h):
@@ -108,7 +110,7 @@ def tile_picked_dhhzarelaypagew_none_p_kernel(
                 )
 
         pick_x_words(0)
-        ws_dealt = keep.tile([P, H], U8, name="ws_dealt", align_bytes=64)
+        ws_dealt = keep.tile([P, H], U8, name="ws_dealt", align_bytes=MX_ALIGN)
 
         def deal_w_scales(tiles):
             nc.vector.tensor_copy(
@@ -116,13 +118,13 @@ def tile_picked_dhhzarelaypagew_none_p_kernel(
                 ws_raw[:].rearrange("p (m t) -> p m t", t=PACK)[:, :, tiles],
             )
 
-        deal_w_scales(slice(0, 2))
+        deal_w_scales(tile_pairs[0])
         pick_x_words(1)
-        deal_w_scales(slice(2, 4))
+        deal_w_scales(tile_pairs[1])
         w_dealt = []
         for a in range(2):
-            dealt = keep.tile([P, H], U32, name=f"w_dealt{a}", tag=f"dealt{a}", align_bytes=64)
-            for tiles in (slice(0, 2), slice(2, 4)):
+            dealt = keep.tile([P, H], U32, name=f"w_dealt{a}", tag=f"dealt{a}", align_bytes=MX_ALIGN)
+            for tiles in tile_pairs:
                 nc.scalar.copy(
                     dealt[:].rearrange("p (t m) -> p m t", t=PACK)[:, :, tiles],
                     w_raw[a][:].bitcast(U32).rearrange("p (m t) -> p m t", t=PACK)[:, :, tiles],
@@ -133,7 +135,7 @@ def tile_picked_dhhzarelaypagew_none_p_kernel(
         n2_t = load_list(n2, "n2_t")
         ka_t = load_list(ka, "ka_t")
         kb_t = load_list(kb, "kb_t")
-        dw_window = keep.tile([P, G], I32, name="dw_window", tag="dw", align_bytes=64)
+        dw_window = keep.tile([P, G], I32, name="dw_window", tag="dw", align_bytes=MX_ALIGN)
         nc.sync.dma_start(dw_window[:], words_view(d_words))
         dsc_window = load_scale_window(d_scales, G, "dsc_window", "raw1")
         gs_t = keep.tile([P, PACK], F32, name="gs_t")
@@ -145,30 +147,29 @@ def tile_picked_dhhzarelaypagew_none_p_kernel(
 
         ds_rows, h_rows, st_rows = [], [], []
         for t in range(PACK):
-            ds_t = keep.tile([P, DS_W], F32, name=f"ds{t}")
+            ds_t = keep.tile([P, DS_WIDTH], F32, name=f"ds{t}")
             nc.vector.memset(ds_t[:, S:], 0.0)
             ds_rows.append(ds_t)
         for t in range(PACK):
-            h_t = keep.tile([P, ROW_W], F32, name=f"h{t}")
+            h_t = keep.tile([P, ROW_WIDTH], F32, name=f"h{t}")
             nc.vector.memset(h_t[:, S:], 0.0)
             h_rows.append(h_t)
-            st_t = keep.tile([P, ROW_W], F32, name=f"st{t}")
+            st_t = keep.tile([P, ROW_WIDTH], F32, name=f"st{t}")
             nc.vector.memset(st_t[:, S:], 0.0)
             st_rows.append(st_t)
 
         y_rows = [keep.tile([P, S], F32, name=f"y{t}") for t in range(PACK)]
-        whole = slice(0, S)
         y_pieces = [(t, cols) for cols in halves for t in (0, 1)] + [(2, whole), (3, whole)]
         for bank, (t, cols) in enumerate(y_pieces):
-            rows = slice(t * P, (t + 1) * P)
+            w_cols = slice(t * P, (t + 1) * P)
             acc = psum.tile([P, cols.stop - cols.start], F32, name=f"y_acc{bank}", tag=f"bank{bank}")
             for h in range(cols.start // HALF, cols.stop // HALF):
-                lo = h * HALF - cols.start
+                first = h * HALF - cols.start
                 for a in (1, 0):
                     nc.tensor.matmul_mx(
-                        out=acc[:, lo : lo + HALF],
-                        lhsT=w_dealt[a][:, rows].bitcast(FP8X4),
-                        lhsT_scale=ws_dealt[4 * a : P, rows],
+                        out=acc[:, first : first + HALF],
+                        lhsT=w_dealt[a][:, w_cols].bitcast(FP8X4),
+                        lhsT_scale=ws_dealt[4 * a : P, w_cols],
                         rhs=xw_picked[:, h, halves[a]].bitcast(FP8X4),
                         rhs_scale=xs_plane[:, h, halves[a]],
                         start=(a == 1),
@@ -177,70 +178,71 @@ def tile_picked_dhhzarelaypagew_none_p_kernel(
             nc.vector.tensor_copy(y_rows[t][:, cols], acc[:])
 
         def pick_d_words(pair, tag):
-            picked = keep.tile([P, 2, 2 * P], U32, name=f"dw_picked{pair}", tag=tag, align_bytes=64)
-            rows = slice(pair * 2 * P, (pair + 1) * 2 * P)
+            picked = keep.tile([P, 2, 2 * P], U32, name=f"dw_picked{pair}", tag=tag, align_bytes=MX_ALIGN)
+            out_rows = slice(pair * 2 * P, (pair + 1) * 2 * P)
             for a, lst in enumerate((ka_t, kb_t)):
-                nc.vector.tensor_copy(picked[:, a, :], dw_window[:].bitcast(U32).indirect(lst[:, entries(rows)]))
+                nc.vector.tensor_copy(picked[:, a, :], dw_window[:].bitcast(U32).indirect(lst[:, entries(out_rows)]))
             return picked
 
         dw_first = pick_d_words(0, "picked")
-        dsc_plane = keep.tile([P, 2 * H], U8, name="dsc_plane", align_bytes=64)
+        dsc_plane = keep.tile([P, 2 * H], U8, name="dsc_plane", align_bytes=MX_ALIGN)
         nc.vector.memset(dsc_plane[:].bitcast(I32), 0)
-        dsc_picked = keep.tile([P, 2 * H], U8, name="dsc_picked", tag="xs_plane", align_bytes=64)
+        dsc_picked = keep.tile([P, 2 * H], U8, name="dsc_picked", tag="xs_plane", align_bytes=MX_ALIGN)
         for a, lst in enumerate((ka_t, kb_t)):
             nc.vector.tensor_copy(dsc_picked[:, a * H : (a + 1) * H], dsc_window[:].indirect(lst[:]))
-        move_scale_rows(dsc_picked, dsc_plane)
+        for j in range(4):
+            source = 16 * (j // 2) + j % 2
+            nc.sync.dma_start(dsc_plane[j:P:32, :].bitcast(I32), dsc_picked[source:P:32, :].bitcast(I32))
 
         fetched = [
-            keep.tile([P, S], F32, name=f"ds_fetched{t}", tag=f"dealt{t}", align_bytes=64) for t in range(PACK)
+            keep.tile([P, S], F32, name=f"ds_fetched{t}", tag=f"dealt{t}", align_bytes=MX_ALIGN) for t in range(PACK)
         ]
-        larger = keep.tile([P, PACK, S], F32, name="larger", tag="raw1", align_bytes=64)
-        z = keep.tile([P, S, PACK], BF16, name="z", align_bytes=64)
-        z_words = keep.tile([P, S], U32, name="z_words", align_bytes=64)
-        z_plane = keep.tile([P, S], U8, name="z_plane", align_bytes=64)
+        larger = keep.tile([P, PACK, S], F32, name="larger", tag="raw1", align_bytes=MX_ALIGN)
+        z = keep.tile([P, S, PACK], BF16, name="z", align_bytes=MX_ALIGN)
+        z_words = keep.tile([P, S], U32, name="z_words", align_bytes=MX_ALIGN)
+        z_plane = keep.tile([P, S], U8, name="z_plane", align_bytes=MX_ALIGN)
 
         def scatter_y(t, cols):
             nc.scalar.activation(ds_rows[t][:].indirect(n1_t[:, entries(cols)]), y_rows[t][:, cols], COPY)
 
-        def make_z(t, lo, hi):
-            nc.scalar.activation(fetched[t][:, lo:hi], ds_rows[t][:].indirect(n2_t[:, lo // 16 : hi // 16]), COPY)
-            nc.vector.tensor_tensor(larger[:, t, lo:hi], y_rows[t][:, lo:hi], fetched[t][:, lo:hi], ALU.max)
-            nc.vector.tensor_scalar(z[:, lo:hi, t], larger[:, t, lo:hi], gs_t[:, t : t + 1], None, ALU.mult)
+        def make_z(t, cols):
+            nc.scalar.activation(fetched[t][:, cols], ds_rows[t][:].indirect(n2_t[:, entries(cols)]), COPY)
+            nc.vector.tensor_tensor(larger[:, t, cols], y_rows[t][:, cols], fetched[t][:, cols], ALU.max)
+            nc.vector.tensor_scalar(z[:, cols, t], larger[:, t, cols], gs_t[:, t : t + 1], None, ALU.mult)
 
-        def quantize_z(lo, hi):
+        last = PACK - 1
+        for t, cols in y_pieces[:-1]:
+            scatter_y(t, cols)
+        for t in range(last):
+            make_z(t, whole)
+        scatter_y(last, whole)
+        for cols in halves:
+            make_z(last, cols)
+        for cols in halves:
             nc.vector.quantize_mx(
-                out=z_words[:, lo:hi].bitcast(FP8X4),
-                scales=z_plane[:, lo:hi],
-                in_=z[:, lo:hi, :].rearrange("p j t -> p (j t)"),
+                out=z_words[:, cols].bitcast(FP8X4),
+                scales=z_plane[:, cols],
+                in_=z[:, cols, :].rearrange("p j t -> p (j t)"),
             )
 
-        for t, cols in y_pieces[:5]:
-            scatter_y(t, cols)
-        for t in range(3):
-            make_z(t, 0, S)
-        scatter_y(3, whole)
-        make_z(3, 0, HALF)
-        make_z(3, HALF, S)
-        quantize_z(0, HALF)
-        quantize_z(HALF, S)
-
         def second_product(t, picked, pieces):
-            for lo, hi, bank in pieces:
-                acc = psum.tile([P, hi - lo], F32, name=f"h_acc{bank}", tag=f"bank{bank}")
+            for cols, bank in pieces:
+                acc = psum.tile([P, cols.stop - cols.start], F32, name=f"h_acc{bank}", tag=f"bank{bank}")
                 for a in range(2):
                     nc.tensor.matmul_mx(
                         out=acc[:],
                         lhsT=picked[:, a, (t % 2) * P : (t % 2 + 1) * P].bitcast(FP8X4),
                         lhsT_scale=dsc_plane[:, a * H + t * P : a * H + (t + 1) * P],
-                        rhs=z_words[:, lo:hi].bitcast(FP8X4),
-                        rhs_scale=z_plane[:, lo:hi],
+                        rhs=z_words[:, cols].bitcast(FP8X4),
+                        rhs_scale=z_plane[:, cols],
                         start=(a == 0),
                         stop=(a == 1),
                     )
-                nc.vector.tensor_scalar(h_rows[t][:, lo:hi], acc[:], 0.0625, None, ALU.mult)
+                nc.vector.tensor_scalar(h_rows[t][:, cols], acc[:], H2_FACTOR, None, ALU.mult)
 
         h_fetched = [
-            keep.tile([P, S], F32, name=f"h_fetched{t}", tag=f"h_fetched{t}", align_bytes=64) for t in range(PACK)
+            keep.tile([P, S], F32, name=f"h_fetched{t}", tag=f"h_fetched{t}", align_bytes=MX_ALIGN)
+            for t in range(PACK)
         ]
         st_fetched = [keep.tile([P, S], F32, name=f"st_fetched{t}") for t in range(PACK)]
         pages = [keep.tile([P, U], F32, name=f"page{t}") for t in range(PACK)]
@@ -260,16 +262,16 @@ def tile_picked_dhhzarelaypagew_none_p_kernel(
             nc.scalar.activation(pages[t][:].indirect(n4_t[:]), up_rows[t], COPY)
             nc.sync.dma_start(out[t * P : (t + 1) * P, :], pages[t][:])
 
-        second_product(0, dw_first, ((0, HALF, 0), (HALF, S, 1)))
-        second_product(1, dw_first, ((0, S, 2),))
+        second_product(0, dw_first, ((halves[0], 0), (halves[1], 1)))
+        second_product(1, dw_first, ((whole, 2),))
         make_st(0)
         make_st(1)
         dw_second = pick_d_words(1, "h_fetched0")
-        second_product(2, dw_second, ((0, S, 3),))
-        second_product(3, dw_second, ((0, S, 4),))
-        up_first = keep.tile([P, 2, S], F32, name="up_first", tag="h_fetched0", align_bytes=64)
+        second_product(2, dw_second, ((whole, 3),))
+        second_product(3, dw_second, ((whole, 4),))
+        up_first = keep.tile([P, 2, S], F32, name="up_first", tag="h_fetched0", align_bytes=MX_ALIGN)
         up_second = keep.tile([P, 2, S], F32, name="up_second")
-        up_rows = [up_first[:, 0, :], up_first[:, 1, :], up_second[:, 0, :], up_second[:, 1, :]]
+        up_rows = [pair[:, i, :] for pair in (up_first, up_second) for i in range(2)]
         for t in (0, 1):
             make_up(t)
             put_st(t)

from contextlib import ExitStack

import concourse.mybir as mybir

K, T, S, H, G, U = 512, 1024, 256, 512, 2048, 512
FLOPS = 2 * 2 * K * H * S + 2 * 2 * K * H * S

F32 = mybir.dt.float32
BF16 = mybir.dt.bfloat16
I32 = mybir.dt.int32
U32 = mybir.dt.uint32
U16 = mybir.dt.uint16
U8 = mybir.dt.uint8
FP8X4 = mybir.dt.float8_e4m3fn_x4
ALU = mybir.AluOpType
COPY = mybir.ActivationFunctionType.Copy

P = 128
PACK = 4
QUADS = 4
BLOCKS = 16
HALF = S // 2
MX_ALIGN = 64
DS_WIDTH = S + HALF
ROW_WIDTH = S + 16
W_SCALES_FIRST = 1
H2_FACTOR = 0.0625


def tile_picked_dhhzarelaypagew_none_p_kernel(
    tc, x_words, x_scales, w1_words, w1_scales, w2_words, w2_scales, gs, d_words, d_scales,
    offs, hz, n1, n2, ka, kb, n3, n4, n5, n6, out,
):
    nc = tc.nc
    halves = (slice(0, HALF), slice(HALF, S))
    whole = slice(0, S)
    tile_pairs = (slice(0, 2), slice(2, 4))

    with ExitStack() as ctx:
        lists = ctx.enter_context(tc.tile_pool(name="lists", bufs=1))
        keep = ctx.enter_context(tc.tile_pool(name="keep", bufs=1))
        psum = ctx.enter_context(tc.psum_pool(name="psum", bufs=1))

        def load_list(src, name):
            tile = lists.tile(list(src.shape), U16, name=name)
            nc.sync.dma_start(tile[:], src)
            return tile

        def entries(span):
            return slice(span.start // 16, span.stop // 16)

        def words_view(words):
            return words[0].rearrange("p n t -> p (n t)").bitcast(I32)

        def load_scale_window(scales, width, name, tag):
            window = keep.tile([P, width], U8, name=name, tag=tag, align_bytes=MX_ALIGN)
            for j in range(2):
                rows = scales[0][j:BLOCKS:2, :].bitcast(I32)
                nc.sync.dma_start(window[j:P:2, :].bitcast(I32), rows.unsqueeze(1).to_broadcast([8, 8, width // 4]))
            return window

        offs_t = load_list(offs, "offs_t")
        hz_t = load_list(hz, "hz_t")
        xs_window = load_scale_window(x_scales, T, "xs_window", "xs_window")

        ws_raw = keep.tile([P, H], U8, name="ws_raw", align_bytes=MX_ALIGN)

        def load_w_scales(a, j):
            rows = (w1_scales, w2_scales)[a][0][j:BLOCKS:4, :].bitcast(I32)
            nc.sync.dma_start(
                ws_raw[4 * a + j : P : 8, :].bitcast(I32), rows.unsqueeze(1).to_broadcast([4, 4, H // 4])
            )

        w_scale_loads = [(a, j) for a in range(2) for j in range(4)]
        for a, j in w_scale_loads[:W_SCALES_FIRST]:
            load_w_scales(a, j)
        xw_window = keep.tile([P, T], I32, name="xw_window", tag="dw", align_bytes=MX_ALIGN)
        nc.sync.dma_start(xw_window[:], words_view(x_words))
        for a, j in w_scale_loads[W_SCALES_FIRST:]:
            load_w_scales(a, j)
        w_raw = []
        for a, words in enumerate((w1_words, w2_words)):
            raw = keep.tile([P, H], I32, name=f"w_raw{a}", tag=f"raw{a}", align_bytes=MX_ALIGN)
            nc.gpsimd.dma_start(raw[:], words_view(words))
            w_raw.append(raw)

        xs_plane = keep.tile([P, 2, 2 * HALF], U8, name="xs_plane", tag="xs_plane", align_bytes=MX_ALIGN)
        nc.vector.memset(xs_plane[:].rearrange("p h s -> p (h s)").bitcast(I32), 0)
        xs_picked = keep.tile([P, 2, 2 * HALF], U8, name="xs_picked", align_bytes=MX_ALIGN)
        xw_picked = keep.tile([P, 2, 2 * HALF], U32, name="xw_picked", tag="picked", align_bytes=MX_ALIGN)

        for h in range(2):
            for a, lst in enumerate((offs_t, hz_t)):
                nc.vector.tensor_copy(xs_picked[:, h, halves[a]], xs_window[:].indirect(lst[:, entries(halves[h])]))
            for j in range(2):
                nc.sync.dma_start(
                    xs_plane[2 + j : P : 32, h, :].bitcast(I32), xs_picked[16 + j : P : 32, h, :].bitcast(I32)
                )
        for q in range(QUADS):
            even_rows = slice(32 * q, 32 * q + 2)
            nc.vector.tensor_copy(
                xs_plane[even_rows, :, :].rearrange("p h s -> p (h s)").bitcast(I32),
                xs_picked[even_rows, :, :].rearrange("p h s -> p (h s)").bitcast(I32),
            )

        def pick_x_words(h):
            for a, lst in enumerate((offs_t, hz_t)):
                nc.vector.tensor_copy(
                    xw_picked[:, h, halves[a]], xw_window[:].bitcast(U32).indirect(lst[:, entries(halves[h])])
                )

        pick_x_words(0)
        ws_dealt = keep.tile([P, H], U8, name="ws_dealt", align_bytes=MX_ALIGN)

        def deal_w_scales(tiles):
            nc.vector.tensor_copy(
                ws_dealt[:].rearrange("p (t m) -> p m t", t=PACK)[:, :, tiles],
                ws_raw[:].rearrange("p (m t) -> p m t", t=PACK)[:, :, tiles],
            )

        deal_w_scales(tile_pairs[0])
        pick_x_words(1)
        deal_w_scales(tile_pairs[1])
        w_dealt = []
        for a in range(2):
            dealt = keep.tile([P, H], U32, name=f"w_dealt{a}", tag=f"dealt{a}", align_bytes=MX_ALIGN)
            for tiles in tile_pairs:
                nc.scalar.copy(
                    dealt[:].rearrange("p (t m) -> p m t", t=PACK)[:, :, tiles],
                    w_raw[a][:].bitcast(U32).rearrange("p (m t) -> p m t", t=PACK)[:, :, tiles],
                )
            w_dealt.append(dealt)

        n1_t = load_list(n1, "n1_t")
        n2_t = load_list(n2, "n2_t")
        ka_t = load_list(ka, "ka_t")
        kb_t = load_list(kb, "kb_t")
        dw_window = keep.tile([P, G], I32, name="dw_window", tag="dw", align_bytes=MX_ALIGN)
        nc.sync.dma_start(dw_window[:], words_view(d_words))
        dsc_window = load_scale_window(d_scales, G, "dsc_window", "raw1")
        gs_t = keep.tile([P, PACK], F32, name="gs_t")
        nc.sync.dma_start(gs_t[:], gs.rearrange("(p t) o -> p (t o)", t=PACK))
        n5_t = load_list(n5, "n5_t")
        n6_t = load_list(n6, "n6_t")
        n3_t = load_list(n3, "n3_t")
        n4_t = load_list(n4, "n4_t")

        ds_rows, h_rows, st_rows = [], [], []
        for t in range(PACK):
            ds_t = keep.tile([P, DS_WIDTH], F32, name=f"ds{t}")
            nc.vector.memset(ds_t[:, S:], 0.0)
            ds_rows.append(ds_t)
        for t in range(PACK):
            h_t = keep.tile([P, ROW_WIDTH], F32, name=f"h{t}")
            nc.vector.memset(h_t[:, S:], 0.0)
            h_rows.append(h_t)
            st_t = keep.tile([P, ROW_WIDTH], F32, name=f"st{t}")
            nc.vector.memset(st_t[:, S:], 0.0)
            st_rows.append(st_t)

        y_rows = [keep.tile([P, S], F32, name=f"y{t}") for t in range(PACK)]
        y_pieces = [(t, cols) for cols in halves for t in (0, 1)] + [(2, whole), (3, whole)]
        for bank, (t, cols) in enumerate(y_pieces):
            w_cols = slice(t * P, (t + 1) * P)
            acc = psum.tile([P, cols.stop - cols.start], F32, name=f"y_acc{bank}", tag=f"bank{bank}")
            for h in range(cols.start // HALF, cols.stop // HALF):
                first = h * HALF - cols.start
                for a in (1, 0):
                    nc.tensor.matmul_mx(
                        out=acc[:, first : first + HALF],
                        lhsT=w_dealt[a][:, w_cols].bitcast(FP8X4),
                        lhsT_scale=ws_dealt[4 * a : P, w_cols],
                        rhs=xw_picked[:, h, halves[a]].bitcast(FP8X4),
                        rhs_scale=xs_plane[:, h, halves[a]],
                        start=(a == 1),
                        stop=(a == 0),
                    )
            nc.vector.tensor_copy(y_rows[t][:, cols], acc[:])

        def pick_d_words(pair, tag):
            picked = keep.tile([P, 2, 2 * P], U32, name=f"dw_picked{pair}", tag=tag, align_bytes=MX_ALIGN)
            out_rows = slice(pair * 2 * P, (pair + 1) * 2 * P)
            for a, lst in enumerate((ka_t, kb_t)):
                nc.vector.tensor_copy(picked[:, a, :], dw_window[:].bitcast(U32).indirect(lst[:, entries(out_rows)]))
            return picked

        dw_first = pick_d_words(0, "picked")
        dsc_plane = keep.tile([P, 2 * H], U8, name="dsc_plane", align_bytes=MX_ALIGN)
        nc.vector.memset(dsc_plane[:].bitcast(I32), 0)
        dsc_picked = keep.tile([P, 2 * H], U8, name="dsc_picked", tag="xs_plane", align_bytes=MX_ALIGN)
        for a, lst in enumerate((ka_t, kb_t)):
            nc.vector.tensor_copy(dsc_picked[:, a * H : (a + 1) * H], dsc_window[:].indirect(lst[:]))
        for j in range(4):
            source = 16 * (j // 2) + j % 2
            nc.sync.dma_start(dsc_plane[j:P:32, :].bitcast(I32), dsc_picked[source:P:32, :].bitcast(I32))

        fetched = [
            keep.tile([P, S], F32, name=f"ds_fetched{t}", tag=f"dealt{t}", align_bytes=MX_ALIGN) for t in range(PACK)
        ]
        larger = keep.tile([P, PACK, S], F32, name="larger", tag="raw1", align_bytes=MX_ALIGN)
        z = keep.tile([P, S, PACK], BF16, name="z", align_bytes=MX_ALIGN)
        z_words = keep.tile([P, S], U32, name="z_words", align_bytes=MX_ALIGN)
        z_plane = keep.tile([P, S], U8, name="z_plane", align_bytes=MX_ALIGN)

        def scatter_y(t, cols):
            nc.scalar.activation(ds_rows[t][:].indirect(n1_t[:, entries(cols)]), y_rows[t][:, cols], COPY)

        def make_z(t, cols):
            nc.scalar.activation(fetched[t][:, cols], ds_rows[t][:].indirect(n2_t[:, entries(cols)]), COPY)
            nc.vector.tensor_tensor(larger[:, t, cols], y_rows[t][:, cols], fetched[t][:, cols], ALU.max)
            nc.vector.tensor_scalar(z[:, cols, t], larger[:, t, cols], gs_t[:, t : t + 1], None, ALU.mult)

        last = PACK - 1
        for t, cols in y_pieces[:-1]:
            scatter_y(t, cols)
        for t in range(last):
            make_z(t, whole)
        scatter_y(last, whole)
        for cols in halves:
            make_z(last, cols)
        for cols in halves:
            nc.vector.quantize_mx(
                out=z_words[:, cols].bitcast(FP8X4),
                scales=z_plane[:, cols],
                in_=z[:, cols, :].rearrange("p j t -> p (j t)"),
            )

        def second_product(t, picked, pieces):
            for cols, bank in pieces:
                acc = psum.tile([P, cols.stop - cols.start], F32, name=f"h_acc{bank}", tag=f"bank{bank}")
                for a in range(2):
                    nc.tensor.matmul_mx(
                        out=acc[:],
                        lhsT=picked[:, a, (t % 2) * P : (t % 2 + 1) * P].bitcast(FP8X4),
                        lhsT_scale=dsc_plane[:, a * H + t * P : a * H + (t + 1) * P],
                        rhs=z_words[:, cols].bitcast(FP8X4),
                        rhs_scale=z_plane[:, cols],
                        start=(a == 0),
                        stop=(a == 1),
                    )
                nc.vector.tensor_scalar(h_rows[t][:, cols], acc[:], H2_FACTOR, None, ALU.mult)

        h_fetched = [
            keep.tile([P, S], F32, name=f"h_fetched{t}", tag=f"h_fetched{t}", align_bytes=MX_ALIGN)
            for t in range(PACK)
        ]
        st_fetched = [keep.tile([P, S], F32, name=f"st_fetched{t}") for t in range(PACK)]
        pages = [keep.tile([P, U], F32, name=f"page{t}") for t in range(PACK)]

        def make_st(t):
            nc.scalar.activation(h_fetched[t][:], h_rows[t][:].indirect(n5_t[:]), COPY)
            nc.vector.tensor_tensor(st_rows[t][:, :S], h_rows[t][:, :S], h_fetched[t][:], ALU.subtract)

        def make_up(t):
            nc.scalar.activation(st_fetched[t][:], st_rows[t][:].indirect(n6_t[:]), COPY)
            nc.vector.tensor_tensor(up_rows[t], st_rows[t][:, :S], st_fetched[t][:], ALU.max)

        def put_st(t):
            nc.scalar.activation(pages[t][:].indirect(n3_t[:]), st_rows[t][:, :S], COPY)

        def put_up(t):
            nc.scalar.activation(pages[t][:].indirect(n4_t[:]), up_rows[t], COPY)
            nc.sync.dma_start(out[t * P : (t + 1) * P, :], pages[t][:])

        second_product(0, dw_first, ((halves[0], 0), (halves[1], 1)))
        second_product(1, dw_first, ((whole, 2),))
        make_st(0)
        make_st(1)
        dw_second = pick_d_words(1, "h_fetched0")
        second_product(2, dw_second, ((whole, 3),))
        second_product(3, dw_second, ((whole, 4),))
        up_first = keep.tile([P, 2, S], F32, name="up_first", tag="h_fetched0", align_bytes=MX_ALIGN)
        up_second = keep.tile([P, 2, S], F32, name="up_second")
        up_rows = [pair[:, i, :] for pair in (up_first, up_second) for i in range(2)]
        for t in (0, 1):
            make_up(t)
            put_st(t)
        make_st(2)
        make_st(3)
        put_up(0)
        put_up(1)
        for t in (2, 3):
            make_up(t)
            put_st(t)
        put_up(2)
        put_up(3)
